import numpy as np
import ml_dtypes


def mxq(x, axis, fmt="e4m3"):
    dtype, down = {"e4m3": (ml_dtypes.float8_e4m3fn, 7), "e5m2": (ml_dtypes.float8_e5m2, 14)}[fmt]
    v = np.moveaxis(np.asarray(x, np.float32).astype(ml_dtypes.bfloat16).astype(np.float64), axis, -1)
    blocks = v.reshape(v.shape[:-1] + (-1, 32))
    amax = np.abs(blocks).max(-1, keepdims=True)
    byte = np.maximum(np.where(amax > 0, np.frexp(amax)[1] - 1 + 127, 0) - down, 1)
    scale = np.exp2(byte - 127.0)
    codes = (blocks / scale).astype(np.float32).astype(dtype).astype(np.float64)
    return np.moveaxis((codes * scale).reshape(v.shape), -1, axis)


WIDE = False


def mx_kscale(k):
    if not WIDE:
        return np.ones(k)
    levels = np.array([10, -10, 5, -5, 0])
    if k % 512:
        return np.exp2(np.random.permutation(np.resize(levels, k // 32))).repeat(32)
    a = np.empty((k // 512, 16))
    for p in range(k // 512):
        a[p, :8] = np.random.permutation(np.resize(levels, 8))
        for g in range(8):
            far = levels[np.abs(levels - a[p, g]) >= 10]
            a[p, g + 8] = far[np.random.randint(len(far))]
    return np.exp2(a.ravel()).repeat(32)


def f64(x):
    return np.asarray(x).astype(np.float64)


def striped(idx):
    return np.tile(np.asarray(idx).reshape(-1, 16).T, (8, 1)).astype(np.uint16)


def unstriped(offs):
    return offs[:16].T.reshape(-1).astype(np.int64)


def striped8(idx):
    return np.asarray(idx).reshape(8, -1, 16).transpose(0, 2, 1).reshape(128, -1).astype(np.uint16)


def unstriped8(offs):
    return offs.reshape(8, 16, -1).transpose(0, 2, 1).reshape(8, -1).astype(np.int64)


def pick8(x, idx, run):
    r = np.arange(len(x))
    return x[r[:, None], idx[r % (8 * run) // run]]


E2M1 = np.array([0.0, 0.5, 1.0, 1.5, 2.0, 3.0, 4.0, 6.0, -0.0, -0.5, -1.0, -1.5, -2.0, -3.0, -4.0, -6.0])


def pack_weight(w, fmt):
    k, n = w.shape
    w = f64(np.asarray(w, np.float32).astype(ml_dtypes.bfloat16)).reshape(k // 32, 32, n)
    amax = np.abs(w).max(1)
    if fmt == "e4m3":
        byte = np.frexp(amax)[1] - 1 + 127 - 7
    else:
        mant, ex = np.frexp(amax / 6.0)
        byte = np.where(mant > 0.5, ex, ex - 1) + 127
    byte = np.clip(np.where(amax > 0, byte, 1), 1, 254)
    scaled = (w * np.exp2(127.0 - byte)[:, None, :]).reshape(k, n).astype(np.float32)
    by_word = np.ascontiguousarray(scaled.reshape(k // 512, 128, 4, n).transpose(0, 1, 3, 2))
    if fmt == "e4m3":
        words = by_word.astype(ml_dtypes.float8_e4m3fn).view(np.uint8)
    else:
        c = by_word.astype(ml_dtypes.float4_e2m1fn).view(np.uint8) & 0xF
        words = (c[..., 0::2] | (c[..., 1::2] << 4)).reshape(k // 512, 128, 2 * n)
    return np.ascontiguousarray(words), np.ascontiguousarray(byte.astype(np.uint8).reshape(k // 512, 16, n))


def unpack_weight(words, scales, fmt):
    g, _, n = scales.shape
    words = np.ascontiguousarray(words).reshape(g, 128, n, -1)
    if fmt == "e4m3":
        vals = words.view(ml_dtypes.float8_e4m3fn).astype(np.float64)
    else:
        nib = np.empty((g, 128, n, 4), np.uint8)
        nib[..., 0::2] = words & 0xF
        nib[..., 1::2] = words >> 4
        vals = E2M1[nib]
    vals = vals * np.repeat(np.exp2(scales.astype(np.float64) - 127.0), 8, axis=1)[..., None]
    return vals.transpose(0, 1, 3, 2).reshape(g * 512, n)


def bf(x):
    return np.asarray(x, np.float32).astype(ml_dtypes.bfloat16)


def planes(Y):
    r, m = Y.shape
    b = f64(bf(Y)).reshape(r // 32, 32, m)
    amax = np.abs(b).max(1)
    byte = np.clip(np.where(amax > 0, np.frexp(amax)[1] - 1 + 127 - 7, 1), 1, 254)
    codes = (b * np.exp2(127.0 - byte)[:, None, :]).reshape(r, m).astype(np.float32).astype(ml_dtypes.float8_e4m3fn).view(np.uint8)
    words = codes.reshape(r // 512, 128, 4, m).transpose(0, 1, 3, 2)
    return np.ascontiguousarray(words), np.ascontiguousarray(byte.astype(np.uint8).reshape(r // 512, 16, m))


K, T, J, S, R, N = 512, 2048, 512, 1024, 512, 512


def setup_inputs():
    n = np.random.standard_normal
    idx = np.random.permutation(T)[:J]
    idx2 = np.stack([np.random.permutation(S)[:J] for _ in range(8)])
    fk = mx_kscale(K)
    fr = mx_kscale(R)
    xtp = pack_weight(n((K, T)) / fk[:, None], "e2m1")
    wap = pack_weight(n((K, R)) * 1 / np.sqrt(K) * fk[:, None] * fr, "e4m3")
    wbp = pack_weight(n((R, N)) * 1 / np.sqrt(R) / fr[:, None], "e2m1")
    return {
        "xt_words": xtp[0],
        "xt_scales": xtp[1],
        "wa_words": wap[0],
        "wa_scales": wap[1],
        "old": (n((R, S)) * 0.7 * fr[:, None]).astype(np.float32),
        "wb_words": wbp[0],
        "wb_scales": wbp[1],
        "offs": striped(idx),
        "offs2": striped8(idx2),
    }


def reference(xt_words, xt_scales, wa_words, wa_scales, old, wb_words, wb_scales, offs, offs2):
    idx = unstriped(offs)
    idx2 = unstriped8(offs2)
    xtu = unpack_weight(xt_words, xt_scales, "e2m1")
    wau = unpack_weight(wa_words, wa_scales, "e4m3")
    wbu = unpack_weight(wb_words, wb_scales, "e2m1")
    xtidxg = xtu[:, idx]
    a = wau.T @ xtidxg
    h1 = np.maximum(a, 0.0)
    hp = np.zeros((R, S))
    hp[np.arange(R)[:, None], idx2[np.arange(R) % 512 // 64]] = h1
    pg = hp + f64(old)
    pgq = mxq(pg, 0, "e4m3")
    y = wbu.T @ pgq
    words, scales = planes(y)
    return y, words, scales

@@ -1,0 +1,222 @@
+from contextlib import ExitStack
+
+import concourse.mybir as mybir
+
+K, T, J, S, R, N = 512, 2048, 512, 1024, 512, 512
+FLOPS = 2 * K * R * J + 2 * R * N * S
+
+F32 = mybir.dt.float32
+BF16 = mybir.dt.bfloat16
+I32 = mybir.dt.int32
+U32 = mybir.dt.uint32
+U16 = mybir.dt.uint16
+U8 = mybir.dt.uint8
+FP8X4 = mybir.dt.float8_e4m3fn_x4
+FP4X4 = mybir.dt.float4_e2m1fn_x4
+ADD = mybir.AluOpType.add
+RELU = mybir.ActivationFunctionType.Relu
+
+P = 128
+PACK = 4
+HALF = J // 2
+BANK = 512
+WIDTHS = (128, 256, 256, 256, 128)
+WEAVE_ON_SCALAR = (1, 3)
+
+
+def load_scale_rows(queue, plane, rows):
+    for q in range(4):
+        queue.dma_start(out=plane[32 * q : 32 * q + 4, :].bitcast(I32), in_=rows[4 * q : 4 * q + 4, :].bitcast(I32))
+
+
+def deal(nc, dealt, natural):
+    nc.vector.tensor_copy(
+        out=dealt.rearrange("p (t m) -> p m t", t=PACK),
+        in_=natural.rearrange("p (m t) -> p m t", t=PACK),
+    )
+
+
+def weave_views(woven, planes):
+    return (
+        woven.rearrange("p (c i t) -> p c t i", i=4, t=PACK),
+        planes.rearrange("p t (c i) -> p c t i", i=4),
+    )
+
+
+def tile_moe_expert_hidden_own_places_pl_kernel(
+    tc, xt_words, xt_scales, wa_words, wa_scales, old, wb_words, wb_scales, offs, offs2, out_0, out_1, out_2
+):
+    nc = tc.nc
+    with ExitStack() as ctx:
+        lists = ctx.enter_context(tc.tile_pool(name="lists", bufs=1))
+        keep = ctx.enter_context(tc.tile_pool(name="keep", bufs=1))
+        pages = ctx.enter_context(tc.tile_pool(name="pages", bufs=3))
+        psum = ctx.enter_context(tc.psum_pool(name="psum", bufs=8))
+
+        tok_list = lists.tile([P, J // 16], U16, name="tok_list")
+        place_list = lists.tile([P, J // 16], U16, name="place_list")
+
+        x_words = keep.tile([P, 2 * T], U8, name="x_words", align_bytes=64)
+        x_plane = keep.tile([P, T], U8, name="x_plane", align_bytes=64)
+        wa_raw = keep.tile([P, R], I32, name="wa_raw", tag="early0", align_bytes=64)
+        wa_plane_raw = keep.tile([P, R], U8, name="wa_plane_raw", tag="early1", align_bytes=64)
+        wb_raw = keep.tile([P, 2 * N], U8, name="wb_raw", align_bytes=64)
+        wb_plane_raw = keep.tile([P, N], U8, name="wb_plane_raw", align_bytes=64)
+
+        nc.vector.memset(x_plane[:].bitcast(I32), 0)
+        nc.vector.memset(wa_plane_raw[:].bitcast(I32), 0)
+        nc.vector.memset(wb_plane_raw[:].bitcast(I32), 0)
+
+        nc.sync.dma_start(out=x_words[:].bitcast(I32), in_=xt_words[0].bitcast(I32))
+        nc.sync.dma_start(tok_list[:], offs)
+        load_scale_rows(nc.scalar, x_plane, xt_scales[0])
+        nc.sync.dma_start(out=wa_raw[:], in_=wa_words[0].rearrange("p c r -> p (c r)").bitcast(I32))
+        load_scale_rows(nc.sync, wa_plane_raw, wa_scales[0])
+        nc.sync.dma_start(place_list[:], offs2)
+        nc.sync.dma_start(out=wb_raw[:].bitcast(I32), in_=wb_words[0].bitcast(I32))
+        load_scale_rows(nc.sync, wb_plane_raw, wb_scales[0])
+
+        page = []
+        for t in range(PACK - 1):
+            page_t = pages.tile([P, S], F32, name="page%d" % t, tag="page")
+            nc.vector.memset(page_t[:], 0.0)
+            page.append(page_t)
+
+        xg_words = []
+        xg_plane = []
+        wa_dealt = keep.tile([P, R], I32, name="wa_dealt", align_bytes=64)
+        wa_plane = keep.tile([P, R], U8, name="wa_plane", align_bytes=64)
+        for h in range(2):
+            entries = tok_list[:, 16 * h : 16 * h + 16]
+            words_h = keep.tile([P, 2 * HALF], U8, name="xg_words%d" % h, align_bytes=64)
+            plane_h = keep.tile([P, HALF], U8, name="xg_plane%d" % h, align_bytes=64)
+            nc.vector.tensor_copy(words_h[:].bitcast(U16), x_words[:].bitcast(U16).indirect(entries))
+            nc.vector.tensor_copy(plane_h[:], x_plane[:].indirect(entries))
+            xg_words.append(words_h)
+            xg_plane.append(plane_h)
+            if h == 0:
+                deal(nc, wa_dealt[:], wa_raw[:])
+                deal(nc, wa_plane[:], wa_plane_raw[:])
+
+        old_rows = old.rearrange("(p t) s -> p t s", t=PACK)
+        old_sb = []
+        for u in range(2):
+            old_u = keep.tile([P, 2, S], F32, name="old%d" % u, tag="early%d" % u, align_bytes=64)
+            nc.sync.dma_start(out=old_u[:], in_=old_rows[:, 2 * u : 2 * u + 2, :])
+            old_sb.extend([old_u[:, 0, :], old_u[:, 1, :]])
+
+        wb_dealt = keep.tile([P, 2 * N], U8, name="wb_dealt", align_bytes=64)
+        wb_plane = keep.tile([P, N], U8, name="wb_plane", align_bytes=64)
+        deal(nc, wb_dealt[:].bitcast(U16), wb_raw[:].bitcast(U16))
+        deal(nc, wb_plane[:], wb_plane_raw[:])
+
+        def first_layer(t, h, acc):
+            cols = slice(P * t, P * (t + 1))
+            nc.tensor.matmul_mx(
+                out=acc,
+                lhsT=wa_dealt[:, cols].bitcast(FP8X4),
+                lhsT_scale=wa_plane[:, cols],
+                rhs=xg_words[h][:].bitcast(FP4X4),
+                rhs_scale=xg_plane[h][:],
+                start=True,
+                stop=True,
+            )
+
+        planes = keep.tile([P, PACK, S], BF16, name="planes", align_bytes=64)
+
+        for h in range(2):
+            for t in range(2):
+                acc = psum.tile([P, BANK], F32, name="acc", tag="bank")
+                first_layer(t, h, acc[:, 0:HALF])
+                hidden = keep.tile([P, HALF], F32, name="hidden%d%d" % (t, h))
+                nc.scalar.activation(out=hidden[:], in_=acc[:, 0:HALF], func=RELU)
+                nc.vector.tensor_copy(page[t][:].indirect(place_list[:, 16 * h : 16 * h + 16]), hidden[:])
+        for t in range(2):
+            nc.gpsimd.tensor_tensor(out=planes[:, t, :], in0=page[t][:], in1=old_sb[t], op=ADD)
+        last_page = pages.tile([P, S], F32, name="page3", tag="page")
+        nc.gpsimd.memset(last_page[:], 0.0)
+        page.append(last_page)
+        for t in range(2, PACK):
+            acc = psum.tile([P, BANK], F32, name="acc", tag="bank")
+            for h in range(2):
+                first_layer(t, h, acc[:, HALF * h : HALF * (h + 1)])
+            hidden = keep.tile([P, J], F32, name="hidden%d" % t)
+            nc.scalar.activation(out=hidden[:], in_=acc[:], func=RELU)
+            nc.vector.tensor_copy(page[t][:].indirect(place_list[:]), hidden[:])
+            if t == 2:
+                nc.gpsimd.tensor_tensor(out=planes[:, t, :], in0=page[t][:], in1=old_sb[t], op=ADD)
+
+        out_rows = out_0.rearrange("(p t) s -> p t s", t=PACK)
+        out_words = out_1[0].rearrange("p c r -> p (c r)").bitcast(I32)
+        y_words = keep.tile([P, S], U32, name="y_words", align_bytes=64)
+        y_plane = keep.tile([P, S], U8, name="y_plane", align_bytes=64)
+        chunks = []
+        for c, width in enumerate(WIDTHS):
+            start = sum(WIDTHS[:c])
+            chunks.append(slice(start, start + width))
+        pg_woven = {}
+        y_sb = {}
+        y_woven = {}
+        banks = {}
+
+        def add_last(c):
+            nc.vector.tensor_tensor(out=planes[:, 3, chunks[c]], in0=page[3][:, chunks[c]], in1=old_sb[3][:, chunks[c]], op=ADD)
+
+        def weave_page(c):
+            woven = keep.tile([P, PACK * WIDTHS[c]], BF16, name="pg_woven%d" % c, align_bytes=64)
+            dst, src = weave_views(woven[:], planes[:, :, chunks[c]])
+            if c in WEAVE_ON_SCALAR:
+                nc.scalar.copy(out=dst, in_=src)
+            else:
+                nc.vector.tensor_copy(out=dst, in_=src)
+            pg_woven[c] = woven
+
+        def second_layer(c):
+            width = WIDTHS[c]
+            words = keep.tile([P, width], U32, name="pg_words%d" % c, align_bytes=64)
+            plane = keep.tile([P, width], U8, name="pg_plane%d" % c, align_bytes=64)
+            nc.vector.quantize_mx(out=words[:].bitcast(FP8X4), scales=plane[:], in_=pg_woven[c][:])
+            per_bank = BANK // width
+            banks[c] = []
+            for t in range(PACK):
+                if t % per_bank == 0:
+                    bank = psum.tile([P, BANK], F32, name="bank", tag="bank")
+                    banks[c].append(bank)
+                at = (t % per_bank) * width
+                nc.tensor.matmul_mx(
+                    out=banks[c][-1][:, at : at + width],
+                    lhsT=wb_dealt[:, 2 * P * t : 2 * P * (t + 1)].bitcast(FP4X4),
+                    lhsT_scale=wb_plane[:, P * t : P * (t + 1)],
+                    rhs=words[:].bitcast(FP8X4),
+                    rhs_scale=plane[:],
+                    start=True,
+                    stop=True,
+                )
+
+        def leave_psum(c):
+            width = WIDTHS[c]
+            y_c = keep.tile([P, PACK * width], F32, name="y%d" % c)
+            for b, bank in enumerate(banks[c]):
+                nc.scalar.copy(out=y_c[:, BANK * b : BANK * (b + 1)], in_=bank[:])
+            nc.sync.dma_start(out=out_rows[:, :, chunks[c]], in_=y_c[:].rearrange("p (t s) -> p t s", t=PACK))
+            y_sb[c] = y_c
+
+        def weave_result(c):
+            woven = keep.tile([P, PACK * WIDTHS[c]], BF16, name="y_woven%d" % c, align_bytes=64)
+            dst, src = weave_views(woven[:], y_sb[c][:].rearrange("p (t s) -> p t s", t=PACK))
+            nc.vector.tensor_copy(out=dst, in_=src)
+            y_woven[c] = woven
+
+        def quantise_result(c):
+            nc.vector.quantize_mx(out=y_words[:, chunks[c]].bitcast(FP8X4), scales=y_plane[:, chunks[c]], in_=y_woven[c][:])
+            nc.sync.dma_start(out=out_words[:, chunks[c]], in_=y_words[:, chunks[c]].bitcast(I32))
+
+        stages = (add_last, weave_page, second_layer, leave_psum, weave_result, quantise_result)
+        for step in range(len(WIDTHS) + len(stages) - 1):
+            for lag, stage in enumerate(stages):
+                if 0 <= step - lag < len(WIDTHS):
+                    stage(step - lag)
+
+        for q in range(4):
+            queue = nc.sync if q % 2 == 0 else nc.scalar
+            queue.dma_start(out=out_2[0][4 * q : 4 * q + 4, :].bitcast(I32), in_=y_plane[32 * q : 32 * q + 4, :].bitcast(I32))

@@ -21,7 +21,8 @@ PACK = 4
 HALF = J // 2
 BANK = 512
 WIDTHS = (128, 256, 256, 256, 128)
-WEAVE_ON_SCALAR = (1, 3)
+WEAVE_ON_SCALAR = (1, 2)
+ROUND_FROM_PSUM = (4,)
 
 
 def load_scale_rows(queue, plane, rows):
@@ -29,10 +30,10 @@ def load_scale_rows(queue, plane, rows):
         queue.dma_start(out=plane[32 * q : 32 * q + 4, :].bitcast(I32), in_=rows[4 * q : 4 * q + 4, :].bitcast(I32))
 
 
-def deal(nc, dealt, natural):
+def deal(nc, dealt, natural, run):
     nc.vector.tensor_copy(
-        out=dealt.rearrange("p (t m) -> p m t", t=PACK),
-        in_=natural.rearrange("p (m t) -> p m t", t=PACK),
+        out=dealt.rearrange("p (t c i) -> p c t i", t=PACK, i=run),
+        in_=natural.rearrange("p (c i t) -> p c t i", t=PACK, i=run),
     )
 
 
@@ -40,6 +41,13 @@ def weave_views(woven, planes):
     return (
         woven.rearrange("p (c i t) -> p c t i", i=4, t=PACK),
         planes.rearrange("p t (c i) -> p c t i", i=4),
+    )
+
+
+def pair_views(woven, planes, u):
+    return (
+        woven.rearrange("p (s t) -> p s t", t=PACK)[:, :, 2 * u : 2 * u + 2],
+        planes[:, 2 * u : 2 * u + 2, :].rearrange("p t s -> p s t"),
     )
 
 
@@ -57,23 +65,21 @@ def tile_moe_expert_hidden_own_places_pl_kernel(
         place_list = lists.tile([P, J // 16], U16, name="place_list")
 
         x_words = keep.tile([P, 2 * T], U8, name="x_words", align_bytes=64)
-        x_plane = keep.tile([P, T], U8, name="x_plane", align_bytes=64)
+        x_plane = keep.tile([P, T], U8, name="x_plane", tag="early2", align_bytes=64)
         wa_raw = keep.tile([P, R], I32, name="wa_raw", tag="early0", align_bytes=64)
         wa_plane_raw = keep.tile([P, R], U8, name="wa_plane_raw", tag="early1", align_bytes=64)
-        wb_raw = keep.tile([P, 2 * N], U8, name="wb_raw", align_bytes=64)
         wb_plane_raw = keep.tile([P, N], U8, name="wb_plane_raw", align_bytes=64)
 
         nc.vector.memset(x_plane[:].bitcast(I32), 0)
         nc.vector.memset(wa_plane_raw[:].bitcast(I32), 0)
         nc.vector.memset(wb_plane_raw[:].bitcast(I32), 0)
 
-        nc.sync.dma_start(out=x_words[:].bitcast(I32), in_=xt_words[0].bitcast(I32))
         nc.sync.dma_start(tok_list[:], offs)
+        nc.sync.dma_start(place_list[:], offs2)
+        nc.sync.dma_start(out=x_words[:].bitcast(I32), in_=xt_words[0].bitcast(I32))
         load_scale_rows(nc.scalar, x_plane, xt_scales[0])
         nc.sync.dma_start(out=wa_raw[:], in_=wa_words[0].rearrange("p c r -> p (c r)").bitcast(I32))
         load_scale_rows(nc.sync, wa_plane_raw, wa_scales[0])
-        nc.sync.dma_start(place_list[:], offs2)
-        nc.sync.dma_start(out=wb_raw[:].bitcast(I32), in_=wb_words[0].bitcast(I32))
         load_scale_rows(nc.sync, wb_plane_raw, wb_scales[0])
 
         page = []
@@ -88,27 +94,28 @@ def tile_moe_expert_hidden_own_places_pl_kernel(
         wa_plane = keep.tile([P, R], U8, name="wa_plane", align_bytes=64)
         for h in range(2):
             entries = tok_list[:, 16 * h : 16 * h + 16]
-            words_h = keep.tile([P, 2 * HALF], U8, name="xg_words%d" % h, align_bytes=64)
+            words_h = keep.tile([P, 2 * HALF], U8, name="xg_words%d" % h, tag=("xg_words0", "early1")[h], align_bytes=64)
             plane_h = keep.tile([P, HALF], U8, name="xg_plane%d" % h, align_bytes=64)
             nc.vector.tensor_copy(words_h[:].bitcast(U16), x_words[:].bitcast(U16).indirect(entries))
             nc.vector.tensor_copy(plane_h[:], x_plane[:].indirect(entries))
             xg_words.append(words_h)
             xg_plane.append(plane_h)
             if h == 0:
-                deal(nc, wa_dealt[:], wa_raw[:])
-                deal(nc, wa_plane[:], wa_plane_raw[:])
+                deal(nc, wa_dealt[:], wa_raw[:], 4)
+                deal(nc, wa_plane[:], wa_plane_raw[:], 16)
 
         old_rows = old.rearrange("(p t) s -> p t s", t=PACK)
-        old_sb = []
+        wb_raw = keep.tile([P, 2 * N], U8, name="wb_raw", tag="early0", align_bytes=64)
+        nc.sync.dma_start(out=wb_raw[:].bitcast(I32), in_=wb_words[0].bitcast(I32))
+        old_all = keep.tile([P, PACK, S], F32, name="old_all", tag="early2", align_bytes=64)
         for u in range(2):
-            old_u = keep.tile([P, 2, S], F32, name="old%d" % u, tag="early%d" % u, align_bytes=64)
-            nc.sync.dma_start(out=old_u[:], in_=old_rows[:, 2 * u : 2 * u + 2, :])
-            old_sb.extend([old_u[:, 0, :], old_u[:, 1, :]])
+            nc.sync.dma_start(out=old_all[:, 2 * u : 2 * u + 2, :], in_=old_rows[:, 2 * u : 2 * u + 2, :])
+        old_sb = [old_all[:, t, :] for t in range(PACK)]
 
         wb_dealt = keep.tile([P, 2 * N], U8, name="wb_dealt", align_bytes=64)
         wb_plane = keep.tile([P, N], U8, name="wb_plane", align_bytes=64)
-        deal(nc, wb_dealt[:].bitcast(U16), wb_raw[:].bitcast(U16))
-        deal(nc, wb_plane[:], wb_plane_raw[:])
+        deal(nc, wb_dealt[:].bitcast(U16), wb_raw[:].bitcast(U16), 8)
+        deal(nc, wb_plane[:], wb_plane_raw[:], 16)
 
         def first_layer(t, h, acc):
             cols = slice(P * t, P * (t + 1))
@@ -124,6 +131,9 @@ def tile_moe_expert_hidden_own_places_pl_kernel(
 
         planes = keep.tile([P, PACK, S], BF16, name="planes", align_bytes=64)
 
+        def add_old(t):
+            nc.gpsimd.tensor_tensor(out=planes[:, t, :], in0=page[t][:], in1=old_sb[t], op=ADD)
+
         for h in range(2):
             for t in range(2):
                 acc = psum.tile([P, BANK], F32, name="acc", tag="bank")
@@ -131,20 +141,22 @@ def tile_moe_expert_hidden_own_places_pl_kernel(
                 hidden = keep.tile([P, HALF], F32, name="hidden%d%d" % (t, h))
                 nc.scalar.activation(out=hidden[:], in_=acc[:, 0:HALF], func=RELU)
                 nc.vector.tensor_copy(page[t][:].indirect(place_list[:, 16 * h : 16 * h + 16]), hidden[:])
-        for t in range(2):
-            nc.gpsimd.tensor_tensor(out=planes[:, t, :], in0=page[t][:], in1=old_sb[t], op=ADD)
-        last_page = pages.tile([P, S], F32, name="page3", tag="page")
-        nc.gpsimd.memset(last_page[:], 0.0)
-        page.append(last_page)
+        late_hidden = {}
         for t in range(2, PACK):
             acc = psum.tile([P, BANK], F32, name="acc", tag="bank")
             for h in range(2):
                 first_layer(t, h, acc[:, HALF * h : HALF * (h + 1)])
             hidden = keep.tile([P, J], F32, name="hidden%d" % t)
             nc.scalar.activation(out=hidden[:], in_=acc[:], func=RELU)
-            nc.vector.tensor_copy(page[t][:].indirect(place_list[:]), hidden[:])
-            if t == 2:
-                nc.gpsimd.tensor_tensor(out=planes[:, t, :], in0=page[t][:], in1=old_sb[t], op=ADD)
+            late_hidden[t] = hidden
+        nc.vector.tensor_copy(page[2][:].indirect(place_list[:]), late_hidden[2][:])
+        add_old(0)
+        last_page = pages.tile([P, S], F32, name="page3", tag="page")
+        nc.gpsimd.memset(last_page[:], 0.0)
+        page.append(last_page)
+        add_old(1)
+        add_old(2)
+        nc.vector.tensor_copy(page[3][:].indirect(place_list[:]), late_hidden[3][:])
 
         out_rows = out_0.rearrange("(p t) s -> p t s", t=PACK)
         out_words = out_1[0].rearrange("p c r -> p (c r)").bitcast(I32)
@@ -155,6 +167,10 @@ def tile_moe_expert_hidden_own_places_pl_kernel(
             start = sum(WIDTHS[:c])
             chunks.append(slice(start, start + width))
         pg_woven = {}
+        for c, width in enumerate(WIDTHS):
+            pg_woven[c] = keep.tile([P, PACK * width], BF16, name="pg_woven%d" % c, align_bytes=64)
+            dst, src = pair_views(pg_woven[c][:], planes[:, :, chunks[c]], 0)
+            nc.scalar.copy(out=dst, in_=src)
         y_sb = {}
         y_woven = {}
         banks = {}
@@ -163,13 +179,11 @@ def tile_moe_expert_hidden_own_places_pl_kernel(
             nc.vector.tensor_tensor(out=planes[:, 3, chunks[c]], in0=page[3][:, chunks[c]], in1=old_sb[3][:, chunks[c]], op=ADD)
 
         def weave_page(c):
-            woven = keep.tile([P, PACK * WIDTHS[c]], BF16, name="pg_woven%d" % c, align_bytes=64)
-            dst, src = weave_views(woven[:], planes[:, :, chunks[c]])
+            dst, src = pair_views(pg_woven[c][:], planes[:, :, chunks[c]], 1)
             if c in WEAVE_ON_SCALAR:
                 nc.scalar.copy(out=dst, in_=src)
             else:
                 nc.vector.tensor_copy(out=dst, in_=src)
-            pg_woven[c] = woven
 
         def second_layer(c):
             width = WIDTHS[c]
@@ -196,12 +210,21 @@ def tile_moe_expert_hidden_own_places_pl_kernel(
         def leave_psum(c):
             width = WIDTHS[c]
             y_c = keep.tile([P, PACK * width], F32, name="y%d" % c)
+            if c in ROUND_FROM_PSUM:
+                woven = keep.tile([P, PACK * width], BF16, name="y_woven%d" % c, align_bytes=64)
+                nc.scalar.copy(
+                    out=woven[:].rearrange("p (s t) -> p s t", t=PACK),
+                    in_=banks[c][0][:].rearrange("p (t s) -> p s t", t=PACK),
+                )
+                y_woven[c] = woven
             for b, bank in enumerate(banks[c]):
                 nc.scalar.copy(out=y_c[:, BANK * b : BANK * (b + 1)], in_=bank[:])
             nc.sync.dma_start(out=out_rows[:, :, chunks[c]], in_=y_c[:].rearrange("p (t s) -> p t s", t=PACK))
             y_sb[c] = y_c
 
         def weave_result(c):
+            if c in ROUND_FROM_PSUM:
+                return
             woven = keep.tile([P, PACK * WIDTHS[c]], BF16, name="y_woven%d" % c, align_bytes=64)
             dst, src = weave_views(woven[:], y_sb[c][:].rearrange("p (t s) -> p t s", t=PACK))
             nc.vector.tensor_copy(out=dst, in_=src)
@@ -211,11 +234,11 @@ def tile_moe_expert_hidden_own_places_pl_kernel(
             nc.vector.quantize_mx(out=y_words[:, chunks[c]].bitcast(FP8X4), scales=y_plane[:, chunks[c]], in_=y_woven[c][:])
             nc.sync.dma_start(out=out_words[:, chunks[c]], in_=y_words[:, chunks[c]].bitcast(I32))
 
-        stages = (add_last, weave_page, second_layer, leave_psum, weave_result, quantise_result)
-        for step in range(len(WIDTHS) + len(stages) - 1):
-            for lag, stage in enumerate(stages):
-                if 0 <= step - lag < len(WIDTHS):
-                    stage(step - lag)
+        for stages in ((add_last, weave_page, second_layer, leave_psum), (weave_result, quantise_result)):
+            for step in range(len(WIDTHS) + len(stages) - 1):
+                for lag, stage in enumerate(stages):
+                    if 0 <= step - lag < len(WIDTHS):
+                        stage(step - lag)
 
         for q in range(4):
             queue = nc.sync if q % 2 == 0 else nc.scalar

from contextlib import ExitStack

import concourse.mybir as mybir

K, T, J, S, R, N = 512, 2048, 512, 1024, 512, 512
FLOPS = 2 * K * R * J + 2 * R * N * S

F32 = mybir.dt.float32
BF16 = mybir.dt.bfloat16
I32 = mybir.dt.int32
U32 = mybir.dt.uint32
U16 = mybir.dt.uint16
U8 = mybir.dt.uint8
FP8X4 = mybir.dt.float8_e4m3fn_x4
FP4X4 = mybir.dt.float4_e2m1fn_x4
ADD = mybir.AluOpType.add
RELU = mybir.ActivationFunctionType.Relu

P = 128
PACK = 4
HALF = J // 2
BANK = 512
WIDTHS = (128, 256, 256, 256, 128)
WEAVE_ON_SCALAR = (1, 2)
ROUND_FROM_PSUM = (4,)


def load_scale_rows(queue, plane, rows):
    for q in range(4):
        queue.dma_start(out=plane[32 * q : 32 * q + 4, :].bitcast(I32), in_=rows[4 * q : 4 * q + 4, :].bitcast(I32))


def deal(nc, dealt, natural, run):
    nc.vector.tensor_copy(
        out=dealt.rearrange("p (t c i) -> p c t i", t=PACK, i=run),
        in_=natural.rearrange("p (c i t) -> p c t i", t=PACK, i=run),
    )


def weave_views(woven, planes):
    return (
        woven.rearrange("p (c i t) -> p c t i", i=4, t=PACK),
        planes.rearrange("p t (c i) -> p c t i", i=4),
    )


def pair_views(woven, planes, u):
    return (
        woven.rearrange("p (s t) -> p s t", t=PACK)[:, :, 2 * u : 2 * u + 2],
        planes[:, 2 * u : 2 * u + 2, :].rearrange("p t s -> p s t"),
    )


def tile_moe_expert_hidden_own_places_pl_kernel(
    tc, xt_words, xt_scales, wa_words, wa_scales, old, wb_words, wb_scales, offs, offs2, out_0, out_1, out_2
):
    nc = tc.nc
    with ExitStack() as ctx:
        lists = ctx.enter_context(tc.tile_pool(name="lists", bufs=1))
        keep = ctx.enter_context(tc.tile_pool(name="keep", bufs=1))
        pages = ctx.enter_context(tc.tile_pool(name="pages", bufs=3))
        psum = ctx.enter_context(tc.psum_pool(name="psum", bufs=8))

        tok_list = lists.tile([P, J // 16], U16, name="tok_list")
        place_list = lists.tile([P, J // 16], U16, name="place_list")

        x_words = keep.tile([P, 2 * T], U8, name="x_words", align_bytes=64)
        x_plane = keep.tile([P, T], U8, name="x_plane", tag="early2", align_bytes=64)
        wa_raw = keep.tile([P, R], I32, name="wa_raw", tag="early0", align_bytes=64)
        wa_plane_raw = keep.tile([P, R], U8, name="wa_plane_raw", tag="early1", align_bytes=64)
        wb_plane_raw = keep.tile([P, N], U8, name="wb_plane_raw", align_bytes=64)

        nc.vector.memset(x_plane[:].bitcast(I32), 0)
        nc.vector.memset(wa_plane_raw[:].bitcast(I32), 0)
        nc.vector.memset(wb_plane_raw[:].bitcast(I32), 0)

        nc.sync.dma_start(tok_list[:], offs)
        nc.sync.dma_start(place_list[:], offs2)
        nc.sync.dma_start(out=x_words[:].bitcast(I32), in_=xt_words[0].bitcast(I32))
        load_scale_rows(nc.scalar, x_plane, xt_scales[0])
        nc.sync.dma_start(out=wa_raw[:], in_=wa_words[0].rearrange("p c r -> p (c r)").bitcast(I32))
        load_scale_rows(nc.sync, wa_plane_raw, wa_scales[0])
        load_scale_rows(nc.sync, wb_plane_raw, wb_scales[0])

        page = []
        for t in range(PACK - 1):
            page_t = pages.tile([P, S], F32, name="page%d" % t, tag="page")
            nc.vector.memset(page_t[:], 0.0)
            page.append(page_t)

        xg_words = []
        xg_plane = []
        wa_dealt = keep.tile([P, R], I32, name="wa_dealt", align_bytes=64)
        wa_plane = keep.tile([P, R], U8, name="wa_plane", align_bytes=64)
        for h in range(2):
            entries = tok_list[:, 16 * h : 16 * h + 16]
            words_h = keep.tile([P, 2 * HALF], U8, name="xg_words%d" % h, tag=("xg_words0", "early1")[h], align_bytes=64)
            plane_h = keep.tile([P, HALF], U8, name="xg_plane%d" % h, align_bytes=64)
            nc.vector.tensor_copy(words_h[:].bitcast(U16), x_words[:].bitcast(U16).indirect(entries))
            nc.vector.tensor_copy(plane_h[:], x_plane[:].indirect(entries))
            xg_words.append(words_h)
            xg_plane.append(plane_h)
            if h == 0:
                deal(nc, wa_dealt[:], wa_raw[:], 4)
                deal(nc, wa_plane[:], wa_plane_raw[:], 16)

        old_rows = old.rearrange("(p t) s -> p t s", t=PACK)
        wb_raw = keep.tile([P, 2 * N], U8, name="wb_raw", tag="early0", align_bytes=64)
        nc.sync.dma_start(out=wb_raw[:].bitcast(I32), in_=wb_words[0].bitcast(I32))
        old_all = keep.tile([P, PACK, S], F32, name="old_all", tag="early2", align_bytes=64)
        for u in range(2):
            nc.sync.dma_start(out=old_all[:, 2 * u : 2 * u + 2, :], in_=old_rows[:, 2 * u : 2 * u + 2, :])
        old_sb = [old_all[:, t, :] for t in range(PACK)]

        wb_dealt = keep.tile([P, 2 * N], U8, name="wb_dealt", align_bytes=64)
        wb_plane = keep.tile([P, N], U8, name="wb_plane", align_bytes=64)
        deal(nc, wb_dealt[:].bitcast(U16), wb_raw[:].bitcast(U16), 8)
        deal(nc, wb_plane[:], wb_plane_raw[:], 16)

        def first_layer(t, h, acc):
            cols = slice(P * t, P * (t + 1))
            nc.tensor.matmul_mx(
                out=acc,
                lhsT=wa_dealt[:, cols].bitcast(FP8X4),
                lhsT_scale=wa_plane[:, cols],
                rhs=xg_words[h][:].bitcast(FP4X4),
                rhs_scale=xg_plane[h][:],
                start=True,
                stop=True,
            )

        planes = keep.tile([P, PACK, S], BF16, name="planes", align_bytes=64)

        def add_old(t):
            nc.gpsimd.tensor_tensor(out=planes[:, t, :], in0=page[t][:], in1=old_sb[t], op=ADD)

        for h in range(2):
            for t in range(2):
                acc = psum.tile([P, BANK], F32, name="acc", tag="bank")
                first_layer(t, h, acc[:, 0:HALF])
                hidden = keep.tile([P, HALF], F32, name="hidden%d%d" % (t, h))
                nc.scalar.activation(out=hidden[:], in_=acc[:, 0:HALF], func=RELU)
                nc.vector.tensor_copy(page[t][:].indirect(place_list[:, 16 * h : 16 * h + 16]), hidden[:])
        late_hidden = {}
        for t in range(2, PACK):
            acc = psum.tile([P, BANK], F32, name="acc", tag="bank")
            for h in range(2):
                first_layer(t, h, acc[:, HALF * h : HALF * (h + 1)])
            hidden = keep.tile([P, J], F32, name="hidden%d" % t)
            nc.scalar.activation(out=hidden[:], in_=acc[:], func=RELU)
            late_hidden[t] = hidden
        nc.vector.tensor_copy(page[2][:].indirect(place_list[:]), late_hidden[2][:])
        add_old(0)
        last_page = pages.tile([P, S], F32, name="page3", tag="page")
        nc.gpsimd.memset(last_page[:], 0.0)
        page.append(last_page)
        add_old(1)
        add_old(2)
        nc.vector.tensor_copy(page[3][:].indirect(place_list[:]), late_hidden[3][:])

        out_rows = out_0.rearrange("(p t) s -> p t s", t=PACK)
        out_words = out_1[0].rearrange("p c r -> p (c r)").bitcast(I32)
        y_words = keep.tile([P, S], U32, name="y_words", align_bytes=64)
        y_plane = keep.tile([P, S], U8, name="y_plane", align_bytes=64)
        chunks = []
        for c, width in enumerate(WIDTHS):
            start = sum(WIDTHS[:c])
            chunks.append(slice(start, start + width))
        pg_woven = {}
        for c, width in enumerate(WIDTHS):
            pg_woven[c] = keep.tile([P, PACK * width], BF16, name="pg_woven%d" % c, align_bytes=64)
            dst, src = pair_views(pg_woven[c][:], planes[:, :, chunks[c]], 0)
            nc.scalar.copy(out=dst, in_=src)
        y_sb = {}
        y_woven = {}
        banks = {}

        def add_last(c):
            nc.vector.tensor_tensor(out=planes[:, 3, chunks[c]], in0=page[3][:, chunks[c]], in1=old_sb[3][:, chunks[c]], op=ADD)

        def weave_page(c):
            dst, src = pair_views(pg_woven[c][:], planes[:, :, chunks[c]], 1)
            if c in WEAVE_ON_SCALAR:
                nc.scalar.copy(out=dst, in_=src)
            else:
                nc.vector.tensor_copy(out=dst, in_=src)

        def second_layer(c):
            width = WIDTHS[c]
            words = keep.tile([P, width], U32, name="pg_words%d" % c, align_bytes=64)
            plane = keep.tile([P, width], U8, name="pg_plane%d" % c, align_bytes=64)
            nc.vector.quantize_mx(out=words[:].bitcast(FP8X4), scales=plane[:], in_=pg_woven[c][:])
            per_bank = BANK // width
            banks[c] = []
            for t in range(PACK):
                if t % per_bank == 0:
                    bank = psum.tile([P, BANK], F32, name="bank", tag="bank")
                    banks[c].append(bank)
                at = (t % per_bank) * width
                nc.tensor.matmul_mx(
                    out=banks[c][-1][:, at : at + width],
                    lhsT=wb_dealt[:, 2 * P * t : 2 * P * (t + 1)].bitcast(FP4X4),
                    lhsT_scale=wb_plane[:, P * t : P * (t + 1)],
                    rhs=words[:].bitcast(FP8X4),
                    rhs_scale=plane[:],
                    start=True,
                    stop=True,
                )

        def leave_psum(c):
            width = WIDTHS[c]
            y_c = keep.tile([P, PACK * width], F32, name="y%d" % c)
            if c in ROUND_FROM_PSUM:
                woven = keep.tile([P, PACK * width], BF16, name="y_woven%d" % c, align_bytes=64)
                nc.scalar.copy(
                    out=woven[:].rearrange("p (s t) -> p s t", t=PACK),
                    in_=banks[c][0][:].rearrange("p (t s) -> p s t", t=PACK),
                )
                y_woven[c] = woven
            for b, bank in enumerate(banks[c]):
                nc.scalar.copy(out=y_c[:, BANK * b : BANK * (b + 1)], in_=bank[:])
            nc.sync.dma_start(out=out_rows[:, :, chunks[c]], in_=y_c[:].rearrange("p (t s) -> p t s", t=PACK))
            y_sb[c] = y_c

        def weave_result(c):
            if c in ROUND_FROM_PSUM:
                return
            woven = keep.tile([P, PACK * WIDTHS[c]], BF16, name="y_woven%d" % c, align_bytes=64)
            dst, src = weave_views(woven[:], y_sb[c][:].rearrange("p (t s) -> p t s", t=PACK))
            nc.vector.tensor_copy(out=dst, in_=src)
            y_woven[c] = woven

        def quantise_result(c):
            nc.vector.quantize_mx(out=y_words[:, chunks[c]].bitcast(FP8X4), scales=y_plane[:, chunks[c]], in_=y_woven[c][:])
            nc.sync.dma_start(out=out_words[:, chunks[c]], in_=y_words[:, chunks[c]].bitcast(I32))

        for stages in ((add_last, weave_page, second_layer, leave_psum), (weave_result, quantise_result)):
            for step in range(len(WIDTHS) + len(stages) - 1):
                for lag, stage in enumerate(stages):
                    if 0 <= step - lag < len(WIDTHS):
                        stage(step - lag)

        for q in range(4):
            queue = nc.sync if q % 2 == 0 else nc.scalar
            queue.dma_start(out=out_2[0][4 * q : 4 * q + 4, :].bitcast(I32), in_=y_plane[32 * q : 32 * q + 4, :].bitcast(I32))
